import numpy as np
import ml_dtypes


def mxq(x, axis, fmt="e4m3"):
    dtype, down = {"e4m3": (ml_dtypes.float8_e4m3fn, 7), "e5m2": (ml_dtypes.float8_e5m2, 14)}[fmt]
    v = np.moveaxis(np.asarray(x, np.float32).astype(ml_dtypes.bfloat16).astype(np.float64), axis, -1)
    blocks = v.reshape(v.shape[:-1] + (-1, 32))
    amax = np.abs(blocks).max(-1, keepdims=True)
    byte = np.maximum(np.where(amax > 0, np.frexp(amax)[1] - 1 + 127, 0) - down, 1)
    scale = np.exp2(byte - 127.0)
    codes = (blocks / scale).astype(np.float32).astype(dtype).astype(np.float64)
    return np.moveaxis((codes * scale).reshape(v.shape), -1, axis)


WIDE = False


def mx_kscale(k):
    if not WIDE:
        return np.ones(k)
    levels = np.array([30, -30])
    if k % 512:
        return np.exp2(np.random.permutation(np.resize(levels, k // 32))).repeat(32)
    a = np.empty((k // 512, 16))
    for p in range(k // 512):
        a[p, :8] = np.random.permutation(np.resize(levels, 8))
        for g in range(8):
            far = levels[np.abs(levels - a[p, g]) >= 10]
            a[p, g + 8] = far[np.random.randint(len(far))]
    return np.exp2(a.ravel()).repeat(32)


def f64(x):
    return np.asarray(x).astype(np.float64)


def striped(idx):
    return np.tile(np.asarray(idx).reshape(-1, 16).T, (8, 1)).astype(np.uint16)


def unstriped(offs):
    return offs[:16].T.reshape(-1).astype(np.int64)


E2M1 = np.array([0.0, 0.5, 1.0, 1.5, 2.0, 3.0, 4.0, 6.0, -0.0, -0.5, -1.0, -1.5, -2.0, -3.0, -4.0, -6.0])


def pack_weight(w, fmt):
    k, n = w.shape
    w = f64(np.asarray(w, np.float32).astype(ml_dtypes.bfloat16)).reshape(k // 32, 32, n)
    amax = np.abs(w).max(1)
    if fmt in ("e4m3", "e5m2"):
        byte = np.frexp(amax)[1] - 1 + 127 - (7 if fmt == "e4m3" else 14)
    else:
        mant, ex = np.frexp(amax / 6.0)
        byte = np.where(mant > 0.5, ex, ex - 1) + 127
    byte = np.clip(np.where(amax > 0, byte, 1), 1, 254)
    scaled = (w * np.exp2(127.0 - byte)[:, None, :]).reshape(k, n).astype(np.float32)
    by_word = np.ascontiguousarray(scaled.reshape(k // 512, 128, 4, n).transpose(0, 1, 3, 2))
    if fmt in ("e4m3", "e5m2"):
        words = by_word.astype(ml_dtypes.float8_e4m3fn if fmt == "e4m3" else ml_dtypes.float8_e5m2).view(np.uint8)
    else:
        c = by_word.astype(ml_dtypes.float4_e2m1fn).view(np.uint8) & 0xF
        words = (c[..., 0::2] | (c[..., 1::2] << 4)).reshape(k // 512, 128, 2 * n)
    return np.ascontiguousarray(words), np.ascontiguousarray(byte.astype(np.uint8).reshape(k // 512, 16, n))


def unpack_weight(words, scales, fmt):
    g, _, n = scales.shape
    words = np.ascontiguousarray(words).reshape(g, 128, n, -1)
    if fmt in ("e4m3", "e5m2"):
        vals = words.view(ml_dtypes.float8_e4m3fn if fmt == "e4m3" else ml_dtypes.float8_e5m2).astype(np.float64)
    else:
        nib = np.empty((g, 128, n, 4), np.uint8)
        nib[..., 0::2] = words & 0xF
        nib[..., 1::2] = words >> 4
        vals = E2M1[nib]
    vals = vals * np.repeat(np.exp2(scales.astype(np.float64) - 127.0), 8, axis=1)[..., None]
    return vals.transpose(0, 1, 3, 2).reshape(g * 512, n)


K, T, Z, J, R, V, N, E = 512, 1024, 1024, 256, 512, 512, 256, 128


def setup_inputs():
    n = np.random.standard_normal
    idx = np.random.permutation(T)[:J]
    idx2 = np.random.permutation(Z)[:J]
    idx3 = np.random.permutation(V)[:J]
    idx4 = np.random.permutation(V)[:J]
    idx5 = np.random.permutation(J)[:E]
    idx6 = np.random.permutation(J)[:E]
    fk = mx_kscale(K)
    fr = mx_kscale(R)
    xtp = pack_weight(n((K, T)) / fk[:, None], "e2m1")
    xop = pack_weight(n((K, Z)) / fk[:, None], "e4m3")
    wp = pack_weight(n((K, R)) * 1 / np.sqrt(K) * fk[:, None] * fr, "e4m3")
    w2p = pack_weight(n((K, R)) * 1 / np.sqrt(K) * fk[:, None] * fr, "e5m2")
    wbp = pack_weight(n((R, N)) * 1 / np.sqrt(R) / fr[:, None], "e2m1")
    return {
        "xt_words": xtp[0],
        "xt_scales": xtp[1],
        "xo_words": xop[0],
        "xo_scales": xop[1],
        "w_words": wp[0],
        "w_scales": wp[1],
        "w2_words": w2p[0],
        "w2_scales": w2p[1],
        "tb": (n((R, V)) * 0.8 * fr[:, None]).astype(np.float32),
        "wb_words": wbp[0],
        "wb_scales": wbp[1],
        "offs": striped(idx),
        "offs2": striped(idx2),
        "offs3": striped(idx3),
        "offs4": striped(idx4),
        "offs5": striped(idx5),
        "offs6": striped(idx6),
    }


def reference(xt_words, xt_scales, xo_words, xo_scales, w_words, w_scales, w2_words, w2_scales, tb, wb_words, wb_scales, offs, offs2, offs3, offs4, offs5, offs6):
    idx = unstriped(offs)
    idx2 = unstriped(offs2)
    idx3 = unstriped(offs3)
    idx4 = unstriped(offs4)
    idx5 = unstriped(offs5)
    idx6 = unstriped(offs6)
    xtu = unpack_weight(xt_words, xt_scales, "e2m1")
    xou = unpack_weight(xo_words, xo_scales, "e4m3")
    wu = unpack_weight(w_words, w_scales, "e4m3")
    w2u = unpack_weight(w2_words, w2_scales, "e5m2")
    wbu = unpack_weight(wb_words, wb_scales, "e2m1")
    xtidxg = xtu[:, idx]
    xoidx2g = xou[:, idx2]
    a = wu.T @ xtidxg + w2u.T @ xoidx2g
    b = w2u.T @ xtidxg + wu.T @ xoidx2g
    hid = np.maximum(a + f64(tb)[:, idx3], b + f64(tb)[:, idx4])
    hidq = mxq(hid, 0, "e5m2")
    p = wbu.T @ hidq
    y = np.maximum(p[:, idx5], p[:, idx6])
    return y

@@ -1,0 +1,211 @@
+from contextlib import ExitStack
+
+import concourse.mybir as mybir
+
+K, T, Z, J, R, V, N, E = 512, 1024, 1024, 256, 512, 512, 256, 128
+FLOPS = 2 * (4 * K * R * J + R * N * J)
+
+F32 = mybir.dt.float32
+BF16 = mybir.dt.bfloat16
+I32 = mybir.dt.int32
+U32 = mybir.dt.uint32
+U16 = mybir.dt.uint16
+U8 = mybir.dt.uint8
+E4M3 = mybir.dt.float8_e4m3fn_x4
+E5M2 = mybir.dt.float8_e5m2_x4
+E2M1 = mybir.dt.float4_e2m1fn_x4
+ADD = mybir.AluOpType.add
+MAX = mybir.AluOpType.max
+COPY = mybir.ActivationFunctionType.Copy
+
+P = 128
+PACK = 4
+ROWS = 16
+HALF = J // 2
+
+XT_AT = 0
+XO_AT = XT_AT + J
+W_AT = XO_AT + J
+W2_AT = W_AT + R
+WB_AT = W2_AT + R
+PLANES = WB_AT + N
+
+
+def tile_list_levelled_crossed_one_bestoftwo_kernel(
+    tc, xt_words, xt_scales, xo_words, xo_scales, w_words, w_scales, w2_words, w2_scales,
+    tb, wb_words, wb_scales, offs, offs2, offs3, offs4, offs5, offs6, out,
+):
+    nc = tc.nc
+    with ExitStack() as ctx:
+        lists = ctx.enter_context(tc.tile_pool(name="lists", bufs=1))
+        sb = ctx.enter_context(tc.tile_pool(name="sb", bufs=1))
+        psum = ctx.enter_context(tc.psum_pool(name="psum", bufs=1))
+
+        def load_list(src, name):
+            held = lists.tile(list(src.shape), U16, name=name)
+            nc.sync.dma_start(held[:], src)
+            return held
+
+        xt_rows = sb.tile([P, T], U8, name="xt_rows", align_bytes=64)
+        xo_rows = sb.tile([P, Z], U8, name="xo_rows", align_bytes=64)
+        w_rows = sb.tile([P, 2 * R], U8, name="w_rows", align_bytes=64)
+        planes = sb.tile([P, PLANES], U8, name="planes", align_bytes=64)
+        nc.vector.memset(xt_rows[:].bitcast(I32), 0)
+        nc.vector.memset(xo_rows[:].bitcast(I32), 0)
+        nc.gpsimd.memset(w_rows[:].bitcast(I32), 0)
+        nc.gpsimd.memset(planes[:, WB_AT:PLANES].bitcast(I32), 0)
+
+        l_xt = load_list(offs, "l_xt")
+        l_xo = load_list(offs2, "l_xo")
+        nc.sync.dma_start(xt_rows[0:ROWS, :].bitcast(I32), xt_scales[0].bitcast(I32))
+        nc.sync.dma_start(xo_rows[0:ROWS, :].bitcast(I32), xo_scales[0].bitcast(I32))
+        nc.sync.dma_start(w_rows[0:ROWS, 0:R].bitcast(I32), w_scales[0].bitcast(I32))
+        nc.sync.dma_start(w_rows[0:ROWS, R : 2 * R].bitcast(I32), w2_scales[0].bitcast(I32))
+
+        xt_all = sb.tile([P, T], U16, name="xt_all", align_bytes=64)
+        xo_all = sb.tile([P, Z], I32, name="xo_all", align_bytes=64)
+        nc.scalar.dma_start(xt_all[:].bitcast(I32), xt_words[0].bitcast(I32))
+        nc.scalar.dma_start(xo_all[:], xo_words[0].rearrange("p c b -> p (c b)").bitcast(I32))
+
+        wb_all = sb.tile([P, 2 * N], U8, name="wb_all", align_bytes=64)
+        nc.gpsimd.dma_start(wb_all[:].bitcast(I32), wb_words[0].bitcast(I32))
+
+        tb_by_t = tb.rearrange("(p t) v -> p t v", t=PACK)
+        levels = [sb.tile([P, V], F32, name=f"levels{t}") for t in range(PACK)]
+        w_raw = [sb.tile([P, R], I32, name=f"w_raw{i}") for i in range(2)]
+        nc.scalar.dma_start(levels[0][:], tb_by_t[:, 0, :])
+        l_tb = [load_list(offs3, "l_tba"), load_list(offs4, "l_tbb")]
+        nc.sync.dma_start(planes[0:ROWS, WB_AT:PLANES].bitcast(I32), wb_scales[0].bitcast(I32))
+        for held, src in zip(w_raw, (w_words, w2_words)):
+            nc.scalar.dma_start(held[:], src[0].rearrange("p c b -> p (c b)").bitcast(I32))
+        for t in range(1, PACK):
+            nc.scalar.dma_start(levels[t][:], tb_by_t[:, t, :])
+        l_p = [load_list(offs5, "l_pa"), load_list(offs6, "l_pb")]
+
+        xt_sc = sb.tile([P, J], U8, name="xt_sc", align_bytes=64)
+        xo_sc = sb.tile([P, J], U8, name="xo_sc", align_bytes=64)
+        nc.vector.tensor_copy(xt_sc[:], xt_rows[:].indirect(l_xt[:]))
+        nc.vector.tensor_copy(xo_sc[:], xo_rows[:].indirect(l_xo[:]))
+        for i in range(2):
+            nc.vector.tensor_copy(
+                planes[:, W_AT + i * R : W_AT + (i + 1) * R].rearrange("p (t c m) -> p c t m", t=PACK, m=16),
+                w_rows[:, i * R : (i + 1) * R].rearrange("p (c m t) -> p c t m", t=PACK, m=16),
+            )
+        nc.vector.tensor_copy(planes[:, XT_AT:XO_AT].bitcast(I32), xt_sc[:].bitcast(I32))
+        nc.vector.tensor_copy(planes[:, XO_AT:W_AT].bitcast(I32), xo_sc[:].bitcast(I32))
+        for q in range(1, 4):
+            nc.sync.dma_start(planes[32 * q : 32 * q + 4, :].bitcast(I32), planes[4 * q : 4 * q + 4, :].bitcast(I32))
+
+        xt_pick = sb.tile([P, J], U16, name="xt_pick", align_bytes=64)
+        xo_pick = sb.tile([P, J], U32, name="xo_pick", align_bytes=64)
+        nc.vector.tensor_copy(xt_pick[:], xt_all[:].indirect(l_xt[:]))
+        nc.vector.tensor_copy(xo_pick[:], xo_all[:].bitcast(U32).indirect(l_xo[:]))
+
+        picked = [sb.tile([P, 2, 2, J], F32, name=f"picked{tp}") for tp in range(2)]
+
+        def pick_level(t, s, on_vector):
+            dst = picked[t // 2][:, s, t % 2, :]
+            src = levels[t][:].indirect(l_tb[s][:])
+            if on_vector:
+                nc.vector.tensor_copy(dst, src)
+            else:
+                nc.scalar.activation(dst, src, COPY)
+
+        pick_level(0, 0, False)
+        pick_level(0, 1, False)
+        w_dealt = [sb.tile([P, R], U32, name=f"w_dealt{i}", align_bytes=64) for i in range(2)]
+        for i in range(2):
+            nc.scalar.copy(
+                w_dealt[i][:].rearrange("p (t c m) -> p c t m", t=PACK, m=4),
+                w_raw[i][:].bitcast(U32).rearrange("p (c m t) -> p c t m", t=PACK, m=4),
+            )
+        pick_level(1, 0, True)
+        pick_level(1, 1, True)
+        pick_level(2, 0, False)
+        pick_level(2, 1, False)
+        pick_level(3, 0, False)
+        pick_level(3, 1, True)
+
+        def weight(i, t):
+            at = W_AT + i * R + t * P
+            return w_dealt[i][:, t * P : (t + 1) * P].bitcast(E4M3 if i == 0 else E5M2), planes[:, at : at + P]
+
+        def picked_x(i, h):
+            cols = slice(h * HALF, (h + 1) * HALF)
+            at = (XT_AT if i == 0 else XO_AT) + h * HALF
+            words = xt_pick[:, cols].bitcast(E2M1) if i == 0 else xo_pick[:, cols].bitcast(E4M3)
+            return words, planes[:, at : at + HALF]
+
+        p_sb = [sb.tile([P, J], F32, name=f"p_sb{g}") for g in range(2)]
+        sums = [sb.tile([P, 2, 2, HALF, 2], F32, name=f"sums{h}") for h in range(2)]
+        hid = [sb.tile([P, HALF * PACK], BF16, name=f"hid{h}", align_bytes=64) for h in range(2)]
+        hid_q = [sb.tile([P, HALF], U32, name=f"hid_q{h}", align_bytes=64) for h in range(2)]
+        hid_sc = [sb.tile([P, HALF], U8, name=f"hid_sc{h}", align_bytes=64) for h in range(2)]
+
+        def first_stage(h, tp):
+            bank = psum.tile([P, 2, 2, HALF], F32, name=f"ab{h}{tp}")
+            for s in range(2):
+                for u in range(2):
+                    for i in range(2):
+                        lhs, lhs_sc = weight((i + s) % 2, 2 * tp + u)
+                        rhs, rhs_sc = picked_x(i, h)
+                        nc.tensor.matmul_mx(
+                            out=bank[:, s, u, :], lhsT=lhs, lhsT_scale=lhs_sc, rhs=rhs, rhs_scale=rhs_sc,
+                            start=(i == 0), stop=(i == 1),
+                        )
+            nc.vector.tensor_tensor(
+                sums[h][:, tp, :, :, :],
+                bank[:].rearrange("p s u j -> p s j u"),
+                picked[tp][:, :, :, h * HALF : (h + 1) * HALF].rearrange("p s u j -> p s j u"),
+                ADD,
+            )
+
+        def larger(h):
+            nc.vector.tensor_tensor(
+                hid[h][:].rearrange("p (j tp u) -> p j tp u", tp=2, u=2),
+                sums[h][:, :, 0, :, :].rearrange("p tp j u -> p j tp u"),
+                sums[h][:, :, 1, :, :].rearrange("p tp j u -> p j tp u"),
+                MAX,
+            )
+
+        def quantise(h):
+            nc.vector.quantize_mx(out=hid_q[h][:].bitcast(E5M2), scales=hid_sc[h][:], in_=hid[h][:])
+
+        def second_stage(h):
+            for g in range(2):
+                bank = psum.tile([P, HALF], F32, name=f"p{h}{g}")
+                nc.tensor.matmul_mx(
+                    out=bank[:],
+                    lhsT=wb_all[:, 2 * g * P : 2 * (g + 1) * P].bitcast(E2M1),
+                    lhsT_scale=planes[:, WB_AT + g * P : WB_AT + (g + 1) * P],
+                    rhs=hid_q[h][:].bitcast(E5M2), rhs_scale=hid_sc[h][:],
+                    start=True, stop=True,
+                )
+                dst = p_sb[g][:, h * HALF : (h + 1) * HALF]
+                if h == 1 and g == 0:
+                    nc.vector.tensor_copy(dst, bank[:])
+                else:
+                    nc.scalar.copy(dst, bank[:])
+
+        first_stage(0, 0)
+        first_stage(0, 1)
+        larger(0)
+        first_stage(1, 0)
+        quantise(0)
+        first_stage(1, 1)
+        second_stage(0)
+        larger(1)
+        quantise(1)
+        second_stage(1)
+
+        for g in range(2):
+            pair = sb.tile([P, 2, E], F32, name=f"pair{g}")
+            for s in range(2):
+                src = p_sb[g][:].indirect(l_p[s][:])
+                if g == 0:
+                    nc.vector.tensor_copy(pair[:, s, :], src)
+                else:
+                    nc.scalar.activation(pair[:, s, :], src, COPY)
+            best = sb.tile([P, E], F32, name=f"best{g}")
+            nc.vector.tensor_tensor(best[:], pair[:, 0, :], pair[:, 1, :], MAX)
+            nc.sync.dma_start(out[g * P : (g + 1) * P, :], best[:])

@@ -21,14 +21,14 @@ COPY = mybir.ActivationFunctionType.Copy
 P = 128
 PACK = 4
 ROWS = 16
+FIRST = P - ROWS
 HALF = J // 2
 
 XT_AT = 0
 XO_AT = XT_AT + J
 W_AT = XO_AT + J
 W2_AT = W_AT + R
-WB_AT = W2_AT + R
-PLANES = WB_AT + N
+PLANES = W2_AT + R
 
 
 def tile_list_levelled_crossed_one_bestoftwo_kernel(
@@ -48,83 +48,102 @@ def tile_list_levelled_crossed_one_bestoftwo_kernel(
 
         xt_rows = sb.tile([P, T], U8, name="xt_rows", align_bytes=64)
         xo_rows = sb.tile([P, Z], U8, name="xo_rows", align_bytes=64)
-        w_rows = sb.tile([P, 2 * R], U8, name="w_rows", align_bytes=64)
+        w_rows = [sb.tile([P, R], U8, name=f"w_rows{i}", tag=f"after_deal{i}", align_bytes=64) for i in range(2)]
         planes = sb.tile([P, PLANES], U8, name="planes", align_bytes=64)
-        nc.vector.memset(xt_rows[:].bitcast(I32), 0)
-        nc.vector.memset(xo_rows[:].bitcast(I32), 0)
-        nc.gpsimd.memset(w_rows[:].bitcast(I32), 0)
-        nc.gpsimd.memset(planes[:, WB_AT:PLANES].bitcast(I32), 0)
+        staged = sb.tile([P, PLANES], U8, name="staged", align_bytes=64)
+        nc.vector.memset(xt_rows[0:FIRST, :].bitcast(I32), 0)
+        nc.vector.memset(xo_rows[0:FIRST, :].bitcast(I32), 0)
+        for held in w_rows:
+            nc.vector.memset(held[0:FIRST, :].bitcast(I32), 0)
+
+        nc.vector.memset(planes[:].bitcast(I32), 0)
 
         l_xt = load_list(offs, "l_xt")
         l_xo = load_list(offs2, "l_xo")
-        nc.sync.dma_start(xt_rows[0:ROWS, :].bitcast(I32), xt_scales[0].bitcast(I32))
-        nc.sync.dma_start(xo_rows[0:ROWS, :].bitcast(I32), xo_scales[0].bitcast(I32))
-        nc.sync.dma_start(w_rows[0:ROWS, 0:R].bitcast(I32), w_scales[0].bitcast(I32))
-        nc.sync.dma_start(w_rows[0:ROWS, R : 2 * R].bitcast(I32), w2_scales[0].bitcast(I32))
+        nc.scalar.dma_start(xt_rows[FIRST:P, :].bitcast(I32), xt_scales[0].bitcast(I32))
+        nc.scalar.dma_start(xo_rows[FIRST:P, :].bitcast(I32), xo_scales[0].bitcast(I32))
+        nc.scalar.dma_start(w_rows[0][FIRST:P, :].bitcast(I32), w_scales[0].bitcast(I32))
+        nc.sync.dma_start(w_rows[1][FIRST:P, :].bitcast(I32), w2_scales[0].bitcast(I32))
+        w_raw = [sb.tile([P, R], I32, name=f"w_raw{i}") for i in range(2)]
+        nc.sync.dma_start(w_raw[0][:], w_words[0].rearrange("p c b -> p (c b)").bitcast(I32))
 
-        xt_all = sb.tile([P, T], U16, name="xt_all", align_bytes=64)
+        xt_all = sb.tile([P, T], U16, name="xt_all", tag="after_tokens", align_bytes=64)
         xo_all = sb.tile([P, Z], I32, name="xo_all", align_bytes=64)
-        nc.scalar.dma_start(xt_all[:].bitcast(I32), xt_words[0].bitcast(I32))
         nc.scalar.dma_start(xo_all[:], xo_words[0].rearrange("p c b -> p (c b)").bitcast(I32))
 
+        tb_by_t = tb.rearrange("(p t) v -> p t v", t=PACK)
+        early_levels = sb.tile([P, 2, V], F32, name="early_levels")
+        nc.gpsimd.dma_start(early_levels[:], tb_by_t[:, 0:2, :])
+        levels = [early_levels[:, 0, :], early_levels[:, 1, :]]
         wb_all = sb.tile([P, 2 * N], U8, name="wb_all", align_bytes=64)
         nc.gpsimd.dma_start(wb_all[:].bitcast(I32), wb_words[0].bitcast(I32))
 
-        tb_by_t = tb.rearrange("(p t) v -> p t v", t=PACK)
-        levels = [sb.tile([P, V], F32, name=f"levels{t}") for t in range(PACK)]
-        w_raw = [sb.tile([P, R], I32, name=f"w_raw{i}") for i in range(2)]
-        nc.scalar.dma_start(levels[0][:], tb_by_t[:, 0, :])
         l_tb = [load_list(offs3, "l_tba"), load_list(offs4, "l_tbb")]
-        nc.sync.dma_start(planes[0:ROWS, WB_AT:PLANES].bitcast(I32), wb_scales[0].bitcast(I32))
-        for held, src in zip(w_raw, (w_words, w2_words)):
-            nc.scalar.dma_start(held[:], src[0].rearrange("p c b -> p (c b)").bitcast(I32))
-        for t in range(1, PACK):
-            nc.scalar.dma_start(levels[t][:], tb_by_t[:, t, :])
         l_p = [load_list(offs5, "l_pa"), load_list(offs6, "l_pb")]
+        nc.sync.dma_start(xt_all[:].bitcast(I32), xt_words[0].bitcast(I32))
+        nc.sync.dma_start(w_raw[1][:], w2_words[0].rearrange("p c b -> p (c b)").bitcast(I32))
 
-        xt_sc = sb.tile([P, J], U8, name="xt_sc", align_bytes=64)
-        xo_sc = sb.tile([P, J], U8, name="xo_sc", align_bytes=64)
+        xt_sc = sb.tile([P, J], U8, name="xt_sc", tag="after_collect", align_bytes=64)
+        xo_sc = sb.tile([P, J], U8, name="xo_sc", tag="late", align_bytes=64)
         nc.vector.tensor_copy(xt_sc[:], xt_rows[:].indirect(l_xt[:]))
         nc.vector.tensor_copy(xo_sc[:], xo_rows[:].indirect(l_xo[:]))
         for i in range(2):
             nc.vector.tensor_copy(
-                planes[:, W_AT + i * R : W_AT + (i + 1) * R].rearrange("p (t c m) -> p c t m", t=PACK, m=16),
-                w_rows[:, i * R : (i + 1) * R].rearrange("p (c m t) -> p c t m", t=PACK, m=16),
+                staged[:, W_AT + i * R : W_AT + (i + 1) * R].rearrange("p (t c m) -> p c t m", t=PACK, m=16),
+                w_rows[i][:].rearrange("p (c m t) -> p c t m", t=PACK, m=16),
             )
-        nc.vector.tensor_copy(planes[:, XT_AT:XO_AT].bitcast(I32), xt_sc[:].bitcast(I32))
-        nc.vector.tensor_copy(planes[:, XO_AT:W_AT].bitcast(I32), xo_sc[:].bitcast(I32))
-        for q in range(1, 4):
-            nc.sync.dma_start(planes[32 * q : 32 * q + 4, :].bitcast(I32), planes[4 * q : 4 * q + 4, :].bitcast(I32))
+        nc.vector.tensor_copy(staged[:, XT_AT:XO_AT].bitcast(I32), xt_sc[:].bitcast(I32))
+        nc.vector.tensor_copy(staged[:, XO_AT:W_AT].bitcast(I32), xo_sc[:].bitcast(I32))
+        for q in range(4):
+            nc.sync.dma_start(
+                planes[32 * q : 32 * q + 4, :].bitcast(I32), staged[FIRST + 4 * q : FIRST + 4 * q + 4, :].bitcast(I32)
+            )
+        late_levels = sb.tile([P, 2, V], F32, name="late_levels", tag="late", align_bytes=64)
+        for u in range(2):
+            nc.sync.dma_start(late_levels[:, u, :], tb_by_t[:, 2 + u, :])
+            levels.append(late_levels[:, u, :])
 
-        xt_pick = sb.tile([P, J], U16, name="xt_pick", align_bytes=64)
-        xo_pick = sb.tile([P, J], U32, name="xo_pick", align_bytes=64)
-        nc.vector.tensor_copy(xt_pick[:], xt_all[:].indirect(l_xt[:]))
-        nc.vector.tensor_copy(xo_pick[:], xo_all[:].bitcast(U32).indirect(l_xo[:]))
+        xt_pick = sb.tile([P, J], U16, name="xt_pick", tag="after_collect", align_bytes=64)
+        xo_pick = sb.tile([P, J], U32, name="xo_pick", tag="after_deal0", align_bytes=64)
 
-        picked = [sb.tile([P, 2, 2, J], F32, name=f"picked{tp}") for tp in range(2)]
+        picked = [
+            sb.tile([P, 2, 2, J], F32, name="picked0", tag="after_deal1", align_bytes=64),
+            sb.tile([P, 2, 2, J], F32, name="picked1"),
+        ]
 
         def pick_level(t, s, on_vector):
             dst = picked[t // 2][:, s, t % 2, :]
-            src = levels[t][:].indirect(l_tb[s][:])
+            src = levels[t].indirect(l_tb[s][:])
             if on_vector:
                 nc.vector.tensor_copy(dst, src)
             else:
                 nc.scalar.activation(dst, src, COPY)
 
-        pick_level(0, 0, False)
-        pick_level(0, 1, False)
         w_dealt = [sb.tile([P, R], U32, name=f"w_dealt{i}", align_bytes=64) for i in range(2)]
-        for i in range(2):
+
+        def deal(i):
             nc.scalar.copy(
                 w_dealt[i][:].rearrange("p (t c m) -> p c t m", t=PACK, m=4),
                 w_raw[i][:].bitcast(U32).rearrange("p (c m t) -> p c t m", t=PACK, m=4),
             )
-        pick_level(1, 0, True)
+
+        nc.vector.tensor_copy(xo_pick[:], xo_all[:].bitcast(U32).indirect(l_xo[:]))
+        deal(0)
+        pick_level(0, 0, False)
+        pick_level(0, 1, True)
+        nc.vector.tensor_copy(xt_pick[:], xt_all[:].indirect(l_xt[:]))
+        pick_level(1, 0, False)
+        deal(1)
         pick_level(1, 1, True)
         pick_level(2, 0, False)
-        pick_level(2, 1, False)
+        pick_level(2, 1, True)
         pick_level(3, 0, False)
-        pick_level(3, 1, True)
+        pick_level(3, 1, False)
+
+        wb_plane = sb.tile([P, N], U8, name="wb_plane", tag="after_tokens", align_bytes=64)
+        nc.vector.memset(wb_plane[:].bitcast(I32), 0)
+        for q in range(4):
+            nc.sync.dma_start(wb_plane[32 * q : 32 * q + 4, :].bitcast(I32), wb_scales[0, 4 * q : 4 * q + 4, :].bitcast(I32))
 
         def weight(i, t):
             at = W_AT + i * R + t * P
@@ -142,20 +161,23 @@ def tile_list_levelled_crossed_one_bestoftwo_kernel(
         hid_q = [sb.tile([P, HALF], U32, name=f"hid_q{h}", align_bytes=64) for h in range(2)]
         hid_sc = [sb.tile([P, HALF], U8, name=f"hid_sc{h}", align_bytes=64) for h in range(2)]
 
-        def first_stage(h, tp):
-            bank = psum.tile([P, 2, 2, HALF], F32, name=f"ab{h}{tp}")
-            for s in range(2):
+        banks = {(h, tp): psum.tile([P, 2, 2, HALF], F32, name=f"ab{h}{tp}") for h in range(2) for tp in range(2)}
+
+        def passes(h, tp, wi):
+            for xi in (1, 0):
+                s = (wi + xi) % 2
                 for u in range(2):
-                    for i in range(2):
-                        lhs, lhs_sc = weight((i + s) % 2, 2 * tp + u)
-                        rhs, rhs_sc = picked_x(i, h)
-                        nc.tensor.matmul_mx(
-                            out=bank[:, s, u, :], lhsT=lhs, lhsT_scale=lhs_sc, rhs=rhs, rhs_scale=rhs_sc,
-                            start=(i == 0), stop=(i == 1),
-                        )
+                    lhs, lhs_sc = weight(wi, 2 * tp + u)
+                    rhs, rhs_sc = picked_x(xi, h)
+                    nc.tensor.matmul_mx(
+                        out=banks[h, tp][:, s, u, :], lhsT=lhs, lhsT_scale=lhs_sc, rhs=rhs, rhs_scale=rhs_sc,
+                        start=(wi == 0 and xi == 1 and u == 0), stop=(wi == 1 and xi == 0 and u == 1),
+                    )
+
+        def add_levels(h, tp):
             nc.vector.tensor_tensor(
                 sums[h][:, tp, :, :, :],
-                bank[:].rearrange("p s u j -> p s j u"),
+                banks[h, tp][:].rearrange("p s u j -> p s j u"),
                 picked[tp][:, :, :, h * HALF : (h + 1) * HALF].rearrange("p s u j -> p s j u"),
                 ADD,
             )
@@ -177,7 +199,7 @@ def tile_list_levelled_crossed_one_bestoftwo_kernel(
                 nc.tensor.matmul_mx(
                     out=bank[:],
                     lhsT=wb_all[:, 2 * g * P : 2 * (g + 1) * P].bitcast(E2M1),
-                    lhsT_scale=planes[:, WB_AT + g * P : WB_AT + (g + 1) * P],
+                    lhsT_scale=wb_plane[:, g * P : (g + 1) * P],
                     rhs=hid_q[h][:].bitcast(E5M2), rhs_scale=hid_sc[h][:],
                     start=True, stop=True,
                 )
@@ -187,15 +209,22 @@ def tile_list_levelled_crossed_one_bestoftwo_kernel(
                 else:
                     nc.scalar.copy(dst, bank[:])
 
-        first_stage(0, 0)
-        first_stage(0, 1)
+        passes(0, 0, 0)
+        passes(1, 0, 0)
+        passes(0, 0, 1)
+        add_levels(0, 0)
+        passes(1, 0, 1)
+        add_levels(1, 0)
+        for h in range(2):
+            passes(h, 1, 0)
+            passes(h, 1, 1)
+        add_levels(0, 1)
+        add_levels(1, 1)
         larger(0)
-        first_stage(1, 0)
-        quantise(0)
-        first_stage(1, 1)
-        second_stage(0)
         larger(1)
+        quantise(0)
         quantise(1)
+        second_stage(0)
         second_stage(1)
 
         for g in range(2):

@@ -20,15 +20,17 @@ COPY = mybir.ActivationFunctionType.Copy
 
 P = 128
 PACK = 4
+QUADRANTS = 4
+QUADRANT = P // QUADRANTS
 ROWS = 16
-FIRST = P - ROWS
+ROWS_AT = P - ROWS
 HALF = J // 2
+LINE = 16
 
 XT_AT = 0
 XO_AT = XT_AT + J
 W_AT = XO_AT + J
-W2_AT = W_AT + R
-PLANES = W2_AT + R
+PLANES = W_AT + 2 * R
 
 
 def tile_list_levelled_crossed_one_bestoftwo_kernel(
@@ -41,6 +43,7 @@ def tile_list_levelled_crossed_one_bestoftwo_kernel(
         sb = ctx.enter_context(tc.tile_pool(name="sb", bufs=1))
         psum = ctx.enter_context(tc.psum_pool(name="psum", bufs=1))
 
+
         def load_list(src, name):
             held = lists.tile(list(src.shape), U16, name=name)
             nc.sync.dma_start(held[:], src)
@@ -51,108 +54,108 @@ def tile_list_levelled_crossed_one_bestoftwo_kernel(
         w_rows = [sb.tile([P, R], U8, name=f"w_rows{i}", tag=f"after_deal{i}", align_bytes=64) for i in range(2)]
         planes = sb.tile([P, PLANES], U8, name="planes", align_bytes=64)
         staged = sb.tile([P, PLANES], U8, name="staged", align_bytes=64)
-        nc.vector.memset(xt_rows[0:FIRST, :].bitcast(I32), 0)
-        nc.vector.memset(xo_rows[0:FIRST, :].bitcast(I32), 0)
-        for held in w_rows:
-            nc.vector.memset(held[0:FIRST, :].bitcast(I32), 0)
-
+        for held in (xt_rows, xo_rows, *w_rows):
+            nc.vector.memset(held[0:ROWS_AT, :].bitcast(I32), 0)
         nc.vector.memset(planes[:].bitcast(I32), 0)
 
+        nc.scalar.dma_start(w_rows[0][ROWS_AT:P, :].bitcast(I32), w_scales[0].bitcast(I32))
         l_xt = load_list(offs, "l_xt")
+        nc.scalar.dma_start(xt_rows[ROWS_AT:P, :].bitcast(I32), xt_scales[0].bitcast(I32))
         l_xo = load_list(offs2, "l_xo")
-        nc.scalar.dma_start(xt_rows[FIRST:P, :].bitcast(I32), xt_scales[0].bitcast(I32))
-        nc.scalar.dma_start(xo_rows[FIRST:P, :].bitcast(I32), xo_scales[0].bitcast(I32))
-        nc.scalar.dma_start(w_rows[0][FIRST:P, :].bitcast(I32), w_scales[0].bitcast(I32))
-        nc.sync.dma_start(w_rows[1][FIRST:P, :].bitcast(I32), w2_scales[0].bitcast(I32))
+        nc.scalar.dma_start(xo_rows[ROWS_AT:P, :].bitcast(I32), xo_scales[0].bitcast(I32))
+        nc.sync.dma_start(w_rows[1][ROWS_AT:P, :].bitcast(I32), w2_scales[0].bitcast(I32))
         w_raw = [sb.tile([P, R], I32, name=f"w_raw{i}") for i in range(2)]
         nc.sync.dma_start(w_raw[0][:], w_words[0].rearrange("p c b -> p (c b)").bitcast(I32))
-
         xt_all = sb.tile([P, T], U16, name="xt_all", tag="after_tokens", align_bytes=64)
-        xo_all = sb.tile([P, Z], I32, name="xo_all", align_bytes=64)
+        xo_all = sb.tile([P, Z], I32, name="xo_all", tag="after_notes", align_bytes=64)
         nc.scalar.dma_start(xo_all[:], xo_words[0].rearrange("p c b -> p (c b)").bitcast(I32))
+        nc.gpsimd.dma_start(xt_all[:].bitcast(I32), xt_words[0].bitcast(I32))
 
         tb_by_t = tb.rearrange("(p t) v -> p t v", t=PACK)
-        early_levels = sb.tile([P, 2, V], F32, name="early_levels")
-        nc.gpsimd.dma_start(early_levels[:], tb_by_t[:, 0:2, :])
-        levels = [early_levels[:, 0, :], early_levels[:, 1, :]]
-        wb_all = sb.tile([P, 2 * N], U8, name="wb_all", align_bytes=64)
-        nc.gpsimd.dma_start(wb_all[:].bitcast(I32), wb_words[0].bitcast(I32))
-
+        early_levels = [
+            sb.tile([P, V], F32, name=f"early_level{t}", tag=f"after_level{t}", align_bytes=64) for t in range(2)
+        ]
+        nc.gpsimd.dma_start(early_levels[1][:], tb_by_t[:, 1, :])
         l_tb = [load_list(offs3, "l_tba"), load_list(offs4, "l_tbb")]
         l_p = [load_list(offs5, "l_pa"), load_list(offs6, "l_pb")]
-        nc.sync.dma_start(xt_all[:].bitcast(I32), xt_words[0].bitcast(I32))
         nc.sync.dma_start(w_raw[1][:], w2_words[0].rearrange("p c b -> p (c b)").bitcast(I32))
+        nc.sync.dma_start(early_levels[0][:], tb_by_t[:, 0, :])
+        levels = [held[:] for held in early_levels]
 
-        xt_sc = sb.tile([P, J], U8, name="xt_sc", tag="after_collect", align_bytes=64)
-        xo_sc = sb.tile([P, J], U8, name="xo_sc", tag="late", align_bytes=64)
+        xt_sc = sb.tile([P, J], U8, name="xt_sc", tag="after_xt_sc", align_bytes=64)
+        xo_sc = sb.tile([P, J], U8, name="xo_sc", tag="after_xo_sc", align_bytes=64)
+
+        def deal_scales(i, engine):
+            engine.tensor_copy(
+                staged[:, W_AT + i * R : W_AT + (i + 1) * R].rearrange("p (t c m) -> p c t m", t=PACK, m=LINE),
+                w_rows[i][:].rearrange("p (c m t) -> p c t m", t=PACK, m=LINE),
+            )
+
+        deal_scales(0, nc.vector)
         nc.vector.tensor_copy(xt_sc[:], xt_rows[:].indirect(l_xt[:]))
         nc.vector.tensor_copy(xo_sc[:], xo_rows[:].indirect(l_xo[:]))
-        for i in range(2):
-            nc.vector.tensor_copy(
-                staged[:, W_AT + i * R : W_AT + (i + 1) * R].rearrange("p (t c m) -> p c t m", t=PACK, m=16),
-                w_rows[i][:].rearrange("p (c m t) -> p c t m", t=PACK, m=16),
-            )
+        deal_scales(1, nc.vector)
         nc.vector.tensor_copy(staged[:, XT_AT:XO_AT].bitcast(I32), xt_sc[:].bitcast(I32))
         nc.vector.tensor_copy(staged[:, XO_AT:W_AT].bitcast(I32), xo_sc[:].bitcast(I32))
-        for q in range(4):
-            nc.sync.dma_start(
-                planes[32 * q : 32 * q + 4, :].bitcast(I32), staged[FIRST + 4 * q : FIRST + 4 * q + 4, :].bitcast(I32)
+        for q in range(QUADRANTS):
+            queue = nc.sync if q % 2 == 0 else nc.scalar
+            rows = slice(ROWS_AT + PACK * q, ROWS_AT + PACK * (q + 1))
+            queue.dma_start(
+                planes[QUADRANT * q : QUADRANT * q + PACK, :].bitcast(I32), staged[rows, :].bitcast(I32)
             )
-        late_levels = sb.tile([P, 2, V], F32, name="late_levels", tag="late", align_bytes=64)
+
+        xt_pick = sb.tile([P, J], U16, name="xt_pick", tag="after_xt_sc", align_bytes=64)
+        xo_pick = sb.tile([P, J], U32, name="xo_pick", tag="after_deal1", align_bytes=64)
+        nc.vector.tensor_copy(xo_pick[:], xo_all[:].bitcast(U32).indirect(l_xo[:]))
+        nc.vector.tensor_copy(xt_pick[:], xt_all[:].indirect(l_xt[:]))
+
+        late_levels = sb.tile([P, 2, V], F32, name="late_levels", tag="after_notes", align_bytes=64)
         for u in range(2):
             nc.sync.dma_start(late_levels[:, u, :], tb_by_t[:, 2 + u, :])
             levels.append(late_levels[:, u, :])
 
-        xt_pick = sb.tile([P, J], U16, name="xt_pick", tag="after_collect", align_bytes=64)
-        xo_pick = sb.tile([P, J], U32, name="xo_pick", tag="after_deal0", align_bytes=64)
-
-        picked = [
-            sb.tile([P, 2, 2, J], F32, name="picked0", tag="after_deal1", align_bytes=64),
-            sb.tile([P, 2, 2, J], F32, name="picked1"),
+        w_dealt = [
+            sb.tile([P, R], U32, name="w_dealt0", align_bytes=64),
+            sb.tile([P, R], U32, name="w_dealt1", tag="after_xo_sc", align_bytes=64),
         ]
-
-        def pick_level(t, s, on_vector):
-            dst = picked[t // 2][:, s, t % 2, :]
-            src = levels[t].indirect(l_tb[s][:])
-            if on_vector:
-                nc.vector.tensor_copy(dst, src)
-            else:
-                nc.scalar.activation(dst, src, COPY)
-
-        w_dealt = [sb.tile([P, R], U32, name=f"w_dealt{i}", align_bytes=64) for i in range(2)]
-
-        def deal(i):
+        for i in range(2):
             nc.scalar.copy(
-                w_dealt[i][:].rearrange("p (t c m) -> p c t m", t=PACK, m=4),
-                w_raw[i][:].bitcast(U32).rearrange("p (c m t) -> p c t m", t=PACK, m=4),
+                w_dealt[i][:].rearrange("p (t c m) -> p c t m", t=PACK, m=LINE // 4),
+                w_raw[i][:].bitcast(U32).rearrange("p (c m t) -> p c t m", t=PACK, m=LINE // 4),
             )
 
-        nc.vector.tensor_copy(xo_pick[:], xo_all[:].bitcast(U32).indirect(l_xo[:]))
-        deal(0)
-        pick_level(0, 0, False)
-        pick_level(0, 1, True)
-        nc.vector.tensor_copy(xt_pick[:], xt_all[:].indirect(l_xt[:]))
-        pick_level(1, 0, False)
-        deal(1)
-        pick_level(1, 1, True)
-        pick_level(2, 0, False)
-        pick_level(2, 1, True)
-        pick_level(3, 0, False)
-        pick_level(3, 1, False)
+        picked = [
+            sb.tile([P, 2, 2, J], F32, name="picked0", tag="after_tokens", align_bytes=64),
+            sb.tile([P, 2, 2, J], F32, name="picked1"),
+        ]
+        for t in range(PACK):
+            for s in range(2):
+                dst = picked[t // 2][:, s, t % 2, :]
+                src = levels[t].indirect(l_tb[s][:])
+                if s == 1 and t < PACK - 1:
+                    nc.vector.tensor_copy(dst, src)
+                else:
+                    nc.scalar.activation(dst, src, COPY)
 
-        wb_plane = sb.tile([P, N], U8, name="wb_plane", tag="after_tokens", align_bytes=64)
-        nc.vector.memset(wb_plane[:].bitcast(I32), 0)
-        for q in range(4):
-            nc.sync.dma_start(wb_plane[32 * q : 32 * q + 4, :].bitcast(I32), wb_scales[0, 4 * q : 4 * q + 4, :].bitcast(I32))
+        wb_both = sb.tile([P, 3 * N], U8, name="wb_both", tag="after_level0", align_bytes=64)
+        wb_all = wb_both[:, 0 : 2 * N]
+        wb_plane = wb_both[:, 2 * N : 3 * N]
+        nc.sync.dma_start(wb_all.bitcast(I32), wb_words[0].bitcast(I32))
+        nc.vector.memset(wb_plane.bitcast(I32), 0)
+        for q in range(QUADRANTS):
+            nc.sync.dma_start(
+                wb_plane[QUADRANT * q : QUADRANT * q + PACK, :].bitcast(I32),
+                wb_scales[0, PACK * q : PACK * (q + 1), :].bitcast(I32),
+            )
 
-        def weight(i, t):
-            at = W_AT + i * R + t * P
-            return w_dealt[i][:, t * P : (t + 1) * P].bitcast(E4M3 if i == 0 else E5M2), planes[:, at : at + P]
+        def weight(wi, t):
+            at = W_AT + wi * R + t * P
+            return w_dealt[wi][:, t * P : (t + 1) * P].bitcast(E4M3 if wi == 0 else E5M2), planes[:, at : at + P]
 
-        def picked_x(i, h):
+        def picked_x(xi, h):
             cols = slice(h * HALF, (h + 1) * HALF)
-            at = (XT_AT if i == 0 else XO_AT) + h * HALF
-            words = xt_pick[:, cols].bitcast(E2M1) if i == 0 else xo_pick[:, cols].bitcast(E4M3)
+            at = (XT_AT if xi == 0 else XO_AT) + h * HALF
+            words = xt_pick[:, cols].bitcast(E2M1) if xi == 0 else xo_pick[:, cols].bitcast(E4M3)
             return words, planes[:, at : at + HALF]
 
         p_sb = [sb.tile([P, J], F32, name=f"p_sb{g}") for g in range(2)]
@@ -161,23 +164,19 @@ def tile_list_levelled_crossed_one_bestoftwo_kernel(
         hid_q = [sb.tile([P, HALF], U32, name=f"hid_q{h}", align_bytes=64) for h in range(2)]
         hid_sc = [sb.tile([P, HALF], U8, name=f"hid_sc{h}", align_bytes=64) for h in range(2)]
 
-        banks = {(h, tp): psum.tile([P, 2, 2, HALF], F32, name=f"ab{h}{tp}") for h in range(2) for tp in range(2)}
-
-        def passes(h, tp, wi):
-            for xi in (1, 0):
-                s = (wi + xi) % 2
-                for u in range(2):
-                    lhs, lhs_sc = weight(wi, 2 * tp + u)
-                    rhs, rhs_sc = picked_x(xi, h)
-                    nc.tensor.matmul_mx(
-                        out=banks[h, tp][:, s, u, :], lhsT=lhs, lhsT_scale=lhs_sc, rhs=rhs, rhs_scale=rhs_sc,
-                        start=(wi == 0 and xi == 1 and u == 0), stop=(wi == 1 and xi == 0 and u == 1),
-                    )
-
-        def add_levels(h, tp):
+        def first_stage(h, tp):
+            bank = psum.tile([P, 2, 2, HALF], F32, name=f"ab{h}{tp}")
+            order = [(wi, xi, u) for wi in range(2) for xi in (1, 0) for u in range(2)]
+            for wi, xi, u in order:
+                lhs, lhs_sc = weight(wi, 2 * tp + u)
+                rhs, rhs_sc = picked_x(xi, h)
+                nc.tensor.matmul_mx(
+                    out=bank[:, (wi + xi) % 2, u, :], lhsT=lhs, lhsT_scale=lhs_sc, rhs=rhs, rhs_scale=rhs_sc,
+                    start=((wi, xi, u) == order[0]), stop=((wi, xi, u) == order[-1]),
+                )
             nc.vector.tensor_tensor(
                 sums[h][:, tp, :, :, :],
-                banks[h, tp][:].rearrange("p s u j -> p s j u"),
+                bank[:].rearrange("p s u j -> p s j u"),
                 picked[tp][:, :, :, h * HALF : (h + 1) * HALF].rearrange("p s u j -> p s j u"),
                 ADD,
             )
@@ -190,10 +189,8 @@ def tile_list_levelled_crossed_one_bestoftwo_kernel(
                 MAX,
             )
 
-        def quantise(h):
-            nc.vector.quantize_mx(out=hid_q[h][:].bitcast(E5M2), scales=hid_sc[h][:], in_=hid[h][:])
-
         def second_stage(h):
+            nc.vector.quantize_mx(out=hid_q[h][:].bitcast(E5M2), scales=hid_sc[h][:], in_=hid[h][:])
             for g in range(2):
                 bank = psum.tile([P, HALF], F32, name=f"p{h}{g}")
                 nc.tensor.matmul_mx(
@@ -209,22 +206,13 @@ def tile_list_levelled_crossed_one_bestoftwo_kernel(
                 else:
                     nc.scalar.copy(dst, bank[:])
 
-        passes(0, 0, 0)
-        passes(1, 0, 0)
-        passes(0, 0, 1)
-        add_levels(0, 0)
-        passes(1, 0, 1)
-        add_levels(1, 0)
-        for h in range(2):
-            passes(h, 1, 0)
-            passes(h, 1, 1)
-        add_levels(0, 1)
-        add_levels(1, 1)
+        first_stage(0, 0)
+        first_stage(1, 0)
+        first_stage(0, 1)
         larger(0)
-        larger(1)
-        quantise(0)
-        quantise(1)
+        first_stage(1, 1)
         second_stage(0)
+        larger(1)
         second_stage(1)
 
         for g in range(2):

@@ -152,40 +152,39 @@ def tile_list_levelled_crossed_one_bestoftwo_kernel(
             at = W_AT + wi * R + t * P
             return w_dealt[wi][:, t * P : (t + 1) * P].bitcast(E4M3 if wi == 0 else E5M2), planes[:, at : at + P]
 
-        def picked_x(xi, h):
-            cols = slice(h * HALF, (h + 1) * HALF)
-            at = (XT_AT if xi == 0 else XO_AT) + h * HALF
-            words = xt_pick[:, cols].bitcast(E2M1) if xi == 0 else xo_pick[:, cols].bitcast(E4M3)
-            return words, planes[:, at : at + HALF]
+        def picked_x(xi):
+            if xi == 0:
+                return xt_pick[:].bitcast(E2M1), planes[:, XT_AT:XO_AT]
+            return xo_pick[:].bitcast(E4M3), planes[:, XO_AT:W_AT]
 
-        p_sb = [sb.tile([P, J], F32, name=f"p_sb{g}") for g in range(2)]
-        sums = [sb.tile([P, 2, 2, HALF, 2], F32, name=f"sums{h}") for h in range(2)]
+        sums = sb.tile([P, 2, 2, J, 2], F32, name="sums")
         hid = [sb.tile([P, HALF * PACK], BF16, name=f"hid{h}", align_bytes=64) for h in range(2)]
         hid_q = [sb.tile([P, HALF], U32, name=f"hid_q{h}", align_bytes=64) for h in range(2)]
         hid_sc = [sb.tile([P, HALF], U8, name=f"hid_sc{h}", align_bytes=64) for h in range(2)]
+        p_sb = [sb.tile([P, J], F32, name=f"p_sb{g}") for g in range(2)]
 
-        def first_stage(h, tp):
-            bank = psum.tile([P, 2, 2, HALF], F32, name=f"ab{h}{tp}")
-            order = [(wi, xi, u) for wi in range(2) for xi in (1, 0) for u in range(2)]
-            for wi, xi, u in order:
-                lhs, lhs_sc = weight(wi, 2 * tp + u)
-                rhs, rhs_sc = picked_x(xi, h)
-                nc.tensor.matmul_mx(
-                    out=bank[:, (wi + xi) % 2, u, :], lhsT=lhs, lhsT_scale=lhs_sc, rhs=rhs, rhs_scale=rhs_sc,
-                    start=((wi, xi, u) == order[0]), stop=((wi, xi, u) == order[-1]),
-                )
+        def first_stage(tp, s):
+            bank = psum.tile([P, 2, J], F32, name=f"ab{tp}{s}")
+            for u in range(2):
+                for wi in range(2):
+                    lhs, lhs_sc = weight(wi, 2 * tp + u)
+                    rhs, rhs_sc = picked_x((wi + s) % 2)
+                    nc.tensor.matmul_mx(
+                        out=bank[:, u, :], lhsT=lhs, lhsT_scale=lhs_sc, rhs=rhs, rhs_scale=rhs_sc,
+                        start=(wi == 0), stop=(wi == 1),
+                    )
             nc.vector.tensor_tensor(
-                sums[h][:, tp, :, :, :],
-                bank[:].rearrange("p s u j -> p s j u"),
-                picked[tp][:, :, :, h * HALF : (h + 1) * HALF].rearrange("p s u j -> p s j u"),
+                sums[:, tp, s, :, :],
+                bank[:].rearrange("p u j -> p j u"),
+                picked[tp][:, s, :, :].rearrange("p u j -> p j u"),
                 ADD,
             )
 
         def larger(h):
             nc.vector.tensor_tensor(
                 hid[h][:].rearrange("p (j tp u) -> p j tp u", tp=2, u=2),
-                sums[h][:, :, 0, :, :].rearrange("p tp j u -> p j tp u"),
-                sums[h][:, :, 1, :, :].rearrange("p tp j u -> p j tp u"),
+                sums[:, :, 0, h * HALF : (h + 1) * HALF, :].rearrange("p tp j u -> p j tp u"),
+                sums[:, :, 1, h * HALF : (h + 1) * HALF, :].rearrange("p tp j u -> p j tp u"),
                 MAX,
             )
 
@@ -206,14 +205,13 @@ def tile_list_levelled_crossed_one_bestoftwo_kernel(
                 else:
                     nc.scalar.copy(dst, bank[:])
 
-        first_stage(0, 0)
-        first_stage(1, 0)
-        first_stage(0, 1)
-        larger(0)
-        first_stage(1, 1)
-        second_stage(0)
-        larger(1)
-        second_stage(1)
+        for tp in range(2):
+            for s in range(2):
+                first_stage(tp, s)
+        for h in range(2):
+            larger(h)
+        for h in range(2):
+            second_stage(h)
 
         for g in range(2):
             pair = sb.tile([P, 2, E], F32, name=f"pair{g}")

from contextlib import ExitStack

import concourse.mybir as mybir

K, T, Z, J, R, V, N, E = 512, 1024, 1024, 256, 512, 512, 256, 128
FLOPS = 2 * (4 * K * R * J + R * N * J)

F32 = mybir.dt.float32
BF16 = mybir.dt.bfloat16
I32 = mybir.dt.int32
U32 = mybir.dt.uint32
U16 = mybir.dt.uint16
U8 = mybir.dt.uint8
E4M3 = mybir.dt.float8_e4m3fn_x4
E5M2 = mybir.dt.float8_e5m2_x4
E2M1 = mybir.dt.float4_e2m1fn_x4
ADD = mybir.AluOpType.add
MAX = mybir.AluOpType.max
COPY = mybir.ActivationFunctionType.Copy

P = 128
PACK = 4
QUADRANTS = 4
QUADRANT = P // QUADRANTS
ROWS = 16
ROWS_AT = P - ROWS
HALF = J // 2
LINE = 16

XT_AT = 0
XO_AT = XT_AT + J
W_AT = XO_AT + J
PLANES = W_AT + 2 * R


def tile_list_levelled_crossed_one_bestoftwo_kernel(
    tc, xt_words, xt_scales, xo_words, xo_scales, w_words, w_scales, w2_words, w2_scales,
    tb, wb_words, wb_scales, offs, offs2, offs3, offs4, offs5, offs6, out,
):
    nc = tc.nc
    with ExitStack() as ctx:
        lists = ctx.enter_context(tc.tile_pool(name="lists", bufs=1))
        sb = ctx.enter_context(tc.tile_pool(name="sb", bufs=1))
        psum = ctx.enter_context(tc.psum_pool(name="psum", bufs=1))


        def load_list(src, name):
            held = lists.tile(list(src.shape), U16, name=name)
            nc.sync.dma_start(held[:], src)
            return held

        xt_rows = sb.tile([P, T], U8, name="xt_rows", align_bytes=64)
        xo_rows = sb.tile([P, Z], U8, name="xo_rows", align_bytes=64)
        w_rows = [sb.tile([P, R], U8, name=f"w_rows{i}", tag=f"after_deal{i}", align_bytes=64) for i in range(2)]
        planes = sb.tile([P, PLANES], U8, name="planes", align_bytes=64)
        staged = sb.tile([P, PLANES], U8, name="staged", align_bytes=64)
        for held in (xt_rows, xo_rows, *w_rows):
            nc.vector.memset(held[0:ROWS_AT, :].bitcast(I32), 0)
        nc.vector.memset(planes[:].bitcast(I32), 0)

        nc.scalar.dma_start(w_rows[0][ROWS_AT:P, :].bitcast(I32), w_scales[0].bitcast(I32))
        l_xt = load_list(offs, "l_xt")
        nc.scalar.dma_start(xt_rows[ROWS_AT:P, :].bitcast(I32), xt_scales[0].bitcast(I32))
        l_xo = load_list(offs2, "l_xo")
        nc.scalar.dma_start(xo_rows[ROWS_AT:P, :].bitcast(I32), xo_scales[0].bitcast(I32))
        nc.sync.dma_start(w_rows[1][ROWS_AT:P, :].bitcast(I32), w2_scales[0].bitcast(I32))
        w_raw = [sb.tile([P, R], I32, name=f"w_raw{i}") for i in range(2)]
        nc.sync.dma_start(w_raw[0][:], w_words[0].rearrange("p c b -> p (c b)").bitcast(I32))
        xt_all = sb.tile([P, T], U16, name="xt_all", tag="after_tokens", align_bytes=64)
        xo_all = sb.tile([P, Z], I32, name="xo_all", tag="after_notes", align_bytes=64)
        nc.scalar.dma_start(xo_all[:], xo_words[0].rearrange("p c b -> p (c b)").bitcast(I32))
        nc.gpsimd.dma_start(xt_all[:].bitcast(I32), xt_words[0].bitcast(I32))

        tb_by_t = tb.rearrange("(p t) v -> p t v", t=PACK)
        early_levels = [
            sb.tile([P, V], F32, name=f"early_level{t}", tag=f"after_level{t}", align_bytes=64) for t in range(2)
        ]
        nc.gpsimd.dma_start(early_levels[1][:], tb_by_t[:, 1, :])
        l_tb = [load_list(offs3, "l_tba"), load_list(offs4, "l_tbb")]
        l_p = [load_list(offs5, "l_pa"), load_list(offs6, "l_pb")]
        nc.sync.dma_start(w_raw[1][:], w2_words[0].rearrange("p c b -> p (c b)").bitcast(I32))
        nc.sync.dma_start(early_levels[0][:], tb_by_t[:, 0, :])
        levels = [held[:] for held in early_levels]

        xt_sc = sb.tile([P, J], U8, name="xt_sc", tag="after_xt_sc", align_bytes=64)
        xo_sc = sb.tile([P, J], U8, name="xo_sc", tag="after_xo_sc", align_bytes=64)

        def deal_scales(i, engine):
            engine.tensor_copy(
                staged[:, W_AT + i * R : W_AT + (i + 1) * R].rearrange("p (t c m) -> p c t m", t=PACK, m=LINE),
                w_rows[i][:].rearrange("p (c m t) -> p c t m", t=PACK, m=LINE),
            )

        deal_scales(0, nc.vector)
        nc.vector.tensor_copy(xt_sc[:], xt_rows[:].indirect(l_xt[:]))
        nc.vector.tensor_copy(xo_sc[:], xo_rows[:].indirect(l_xo[:]))
        deal_scales(1, nc.vector)
        nc.vector.tensor_copy(staged[:, XT_AT:XO_AT].bitcast(I32), xt_sc[:].bitcast(I32))
        nc.vector.tensor_copy(staged[:, XO_AT:W_AT].bitcast(I32), xo_sc[:].bitcast(I32))
        for q in range(QUADRANTS):
            queue = nc.sync if q % 2 == 0 else nc.scalar
            rows = slice(ROWS_AT + PACK * q, ROWS_AT + PACK * (q + 1))
            queue.dma_start(
                planes[QUADRANT * q : QUADRANT * q + PACK, :].bitcast(I32), staged[rows, :].bitcast(I32)
            )

        xt_pick = sb.tile([P, J], U16, name="xt_pick", tag="after_xt_sc", align_bytes=64)
        xo_pick = sb.tile([P, J], U32, name="xo_pick", tag="after_deal1", align_bytes=64)
        nc.vector.tensor_copy(xo_pick[:], xo_all[:].bitcast(U32).indirect(l_xo[:]))
        nc.vector.tensor_copy(xt_pick[:], xt_all[:].indirect(l_xt[:]))

        late_levels = sb.tile([P, 2, V], F32, name="late_levels", tag="after_notes", align_bytes=64)
        for u in range(2):
            nc.sync.dma_start(late_levels[:, u, :], tb_by_t[:, 2 + u, :])
            levels.append(late_levels[:, u, :])

        w_dealt = [
            sb.tile([P, R], U32, name="w_dealt0", align_bytes=64),
            sb.tile([P, R], U32, name="w_dealt1", tag="after_xo_sc", align_bytes=64),
        ]
        for i in range(2):
            nc.scalar.copy(
                w_dealt[i][:].rearrange("p (t c m) -> p c t m", t=PACK, m=LINE // 4),
                w_raw[i][:].bitcast(U32).rearrange("p (c m t) -> p c t m", t=PACK, m=LINE // 4),
            )

        picked = [
            sb.tile([P, 2, 2, J], F32, name="picked0", tag="after_tokens", align_bytes=64),
            sb.tile([P, 2, 2, J], F32, name="picked1"),
        ]
        for t in range(PACK):
            for s in range(2):
                dst = picked[t // 2][:, s, t % 2, :]
                src = levels[t].indirect(l_tb[s][:])
                if s == 1 and t < PACK - 1:
                    nc.vector.tensor_copy(dst, src)
                else:
                    nc.scalar.activation(dst, src, COPY)

        wb_both = sb.tile([P, 3 * N], U8, name="wb_both", tag="after_level0", align_bytes=64)
        wb_all = wb_both[:, 0 : 2 * N]
        wb_plane = wb_both[:, 2 * N : 3 * N]
        nc.sync.dma_start(wb_all.bitcast(I32), wb_words[0].bitcast(I32))
        nc.vector.memset(wb_plane.bitcast(I32), 0)
        for q in range(QUADRANTS):
            nc.sync.dma_start(
                wb_plane[QUADRANT * q : QUADRANT * q + PACK, :].bitcast(I32),
                wb_scales[0, PACK * q : PACK * (q + 1), :].bitcast(I32),
            )

        def weight(wi, t):
            at = W_AT + wi * R + t * P
            return w_dealt[wi][:, t * P : (t + 1) * P].bitcast(E4M3 if wi == 0 else E5M2), planes[:, at : at + P]

        def picked_x(xi):
            if xi == 0:
                return xt_pick[:].bitcast(E2M1), planes[:, XT_AT:XO_AT]
            return xo_pick[:].bitcast(E4M3), planes[:, XO_AT:W_AT]

        sums = sb.tile([P, 2, 2, J, 2], F32, name="sums")
        hid = [sb.tile([P, HALF * PACK], BF16, name=f"hid{h}", align_bytes=64) for h in range(2)]
        hid_q = [sb.tile([P, HALF], U32, name=f"hid_q{h}", align_bytes=64) for h in range(2)]
        hid_sc = [sb.tile([P, HALF], U8, name=f"hid_sc{h}", align_bytes=64) for h in range(2)]
        p_sb = [sb.tile([P, J], F32, name=f"p_sb{g}") for g in range(2)]

        def first_stage(tp, s):
            bank = psum.tile([P, 2, J], F32, name=f"ab{tp}{s}")
            for u in range(2):
                for wi in range(2):
                    lhs, lhs_sc = weight(wi, 2 * tp + u)
                    rhs, rhs_sc = picked_x((wi + s) % 2)
                    nc.tensor.matmul_mx(
                        out=bank[:, u, :], lhsT=lhs, lhsT_scale=lhs_sc, rhs=rhs, rhs_scale=rhs_sc,
                        start=(wi == 0), stop=(wi == 1),
                    )
            nc.vector.tensor_tensor(
                sums[:, tp, s, :, :],
                bank[:].rearrange("p u j -> p j u"),
                picked[tp][:, s, :, :].rearrange("p u j -> p j u"),
                ADD,
            )

        def larger(h):
            nc.vector.tensor_tensor(
                hid[h][:].rearrange("p (j tp u) -> p j tp u", tp=2, u=2),
                sums[:, :, 0, h * HALF : (h + 1) * HALF, :].rearrange("p tp j u -> p j tp u"),
                sums[:, :, 1, h * HALF : (h + 1) * HALF, :].rearrange("p tp j u -> p j tp u"),
                MAX,
            )

        def second_stage(h):
            nc.vector.quantize_mx(out=hid_q[h][:].bitcast(E5M2), scales=hid_sc[h][:], in_=hid[h][:])
            for g in range(2):
                bank = psum.tile([P, HALF], F32, name=f"p{h}{g}")
                nc.tensor.matmul_mx(
                    out=bank[:],
                    lhsT=wb_all[:, 2 * g * P : 2 * (g + 1) * P].bitcast(E2M1),
                    lhsT_scale=wb_plane[:, g * P : (g + 1) * P],
                    rhs=hid_q[h][:].bitcast(E5M2), rhs_scale=hid_sc[h][:],
                    start=True, stop=True,
                )
                dst = p_sb[g][:, h * HALF : (h + 1) * HALF]
                if h == 1 and g == 0:
                    nc.vector.tensor_copy(dst, bank[:])
                else:
                    nc.scalar.copy(dst, bank[:])

        for tp in range(2):
            for s in range(2):
                first_stage(tp, s)
        for h in range(2):
            larger(h)
        for h in range(2):
            second_stage(h)

        for g in range(2):
            pair = sb.tile([P, 2, E], F32, name=f"pair{g}")
            for s in range(2):
                src = p_sb[g][:].indirect(l_p[s][:])
                if g == 0:
                    nc.vector.tensor_copy(pair[:, s, :], src)
                else:
                    nc.scalar.activation(pair[:, s, :], src, COPY)
            best = sb.tile([P, E], F32, name=f"best{g}")
            nc.vector.tensor_tensor(best[:], pair[:, 0, :], pair[:, 1, :], MAX)
            nc.sync.dma_start(out[g * P : (g + 1) * P, :], best[:])
